import numpy as np
import ml_dtypes


def mxq(x, axis, fmt="e4m3"):
    dtype, down = {"e4m3": (ml_dtypes.float8_e4m3fn, 7), "e5m2": (ml_dtypes.float8_e5m2, 14)}[fmt]
    v = np.moveaxis(np.asarray(x, np.float32).astype(ml_dtypes.bfloat16).astype(np.float64), axis, -1)
    blocks = v.reshape(v.shape[:-1] + (-1, 32))
    amax = np.abs(blocks).max(-1, keepdims=True)
    byte = np.maximum(np.where(amax > 0, np.frexp(amax)[1] - 1 + 127, 0) - down, 1)
    scale = np.exp2(byte - 127.0)
    codes = (blocks / scale).astype(np.float32).astype(dtype).astype(np.float64)
    return np.moveaxis((codes * scale).reshape(v.shape), -1, axis)


WIDE = False


def mx_kscale(k):
    if not WIDE:
        return np.ones(k)
    levels = np.array([10, -10, 5, -5, 0])
    if k % 512:
        return np.exp2(np.random.permutation(np.resize(levels, k // 32))).repeat(32)
    a = np.empty((k // 512, 16))
    for p in range(k // 512):
        a[p, :8] = np.random.permutation(np.resize(levels, 8))
        for g in range(8):
            far = levels[np.abs(levels - a[p, g]) >= 10]
            a[p, g + 8] = far[np.random.randint(len(far))]
    return np.exp2(a.ravel()).repeat(32)


def f64(x):
    return np.asarray(x).astype(np.float64)


def striped(idx):
    return np.tile(idx.reshape(-1, 16).T, (8, 1)).astype(np.uint16)


def unstriped(offs):
    return offs[:16].T.reshape(-1).astype(np.int64)


def pack_weight(w):
    k, n = w.shape
    w = f64(np.asarray(w, np.float32).astype(ml_dtypes.bfloat16)).reshape(k // 32, 32, n)
    amax = np.abs(w).max(1)
    byte = np.clip(np.where(amax > 0, np.frexp(amax)[1] - 1 + 127 - 7, 1), 1, 254)
    scaled = (w * np.exp2(127.0 - byte)[:, None, :]).reshape(k, n).astype(np.float32)
    words = np.ascontiguousarray(scaled.reshape(k // 512, 128, 4, n).transpose(0, 1, 3, 2)).astype(ml_dtypes.float8_e4m3fn).view(np.uint8)
    return words, np.ascontiguousarray(byte.astype(np.uint8).reshape(k // 512, 16, n))


def unpack_weight(words, scales):
    g, p, n, _ = words.shape
    vals = np.ascontiguousarray(words).view(ml_dtypes.float8_e4m3fn).astype(np.float64) * np.repeat(np.exp2(scales.astype(np.float64) - 127.0), 8, axis=1)[..., None]
    return vals.transpose(0, 1, 3, 2).reshape(g * 512, n)


E2M1 = np.array([0.0, 0.5, 1.0, 1.5, 2.0, 3.0, 4.0, 6.0, -0.0, -0.5, -1.0, -1.5, -2.0, -3.0, -4.0, -6.0])


def pack_fp4(w):
    k, n = w.shape
    w = f64(np.asarray(w, np.float32).astype(ml_dtypes.bfloat16)).reshape(k // 32, 32, n)
    amax = np.abs(w).max(1)
    mant, ex = np.frexp(amax / 6.0)
    byte = np.clip(np.where(amax > 0, np.where(mant > 0.5, ex, ex - 1) + 127, 1), 1, 254)
    scaled = (w * np.exp2(127.0 - byte)[:, None, :]).reshape(k, n).astype(np.float32)
    c = np.ascontiguousarray(scaled.reshape(k // 512, 128, 4, n).transpose(0, 1, 3, 2)).astype(ml_dtypes.float4_e2m1fn).view(np.uint8) & 0xF
    words = (c[..., 0::2] | (c[..., 1::2] << 4)).reshape(k // 512, 128, 2 * n)
    return np.ascontiguousarray(words), np.ascontiguousarray(byte.astype(np.uint8).reshape(k // 512, 16, n))


def unpack_fp4(words, scales):
    g, _, n = scales.shape
    words = np.ascontiguousarray(words).reshape(g, 128, n, 2)
    nib = np.empty((g, 128, n, 4), np.uint8)
    nib[..., 0::2] = words & 0xF
    nib[..., 1::2] = words >> 4
    vals = E2M1[nib] * np.repeat(np.exp2(scales.astype(np.float64) - 127.0), 8, axis=1)[..., None]
    return vals.transpose(0, 1, 3, 2).reshape(g * 512, n)


K, T, S, N, H, U, W = 512, 1024, 512, 128, 512, 1024, 512


def setup_inputs():
    n = np.random.standard_normal
    s = mx_kscale(K)[:, None]
    u = mx_kscale(H)
    near = np.random.permutation(U)
    packed_xT = pack_weight(n((K, T)) * s)
    packed_w1 = pack_fp4(n((K, H)) / np.sqrt(K) / s)
    packed_w2 = pack_fp4(n((H, N)) / np.sqrt(H) / u[:, None])
    return {
        "x_words": packed_xT[0],
        "x_scales": packed_xT[1],
        "w1_words": packed_w1[0],
        "w1_scales": packed_w1[1],
        "grid": (n((H, U))).astype(np.float32),
        "rob": (np.random.uniform(0.3, 0.9, (H, 1))).astype(np.float32),
        "unit": (np.random.uniform(0.6, 1.4, (H, 1)) * u[:, None]).astype(np.float32),
        "w2_words": packed_w2[0],
        "w2_scales": packed_w2[1],
        "offs": striped(np.random.permutation(T)[:S]),
        "gh": striped(np.random.permutation(U)[:S]),
        "inn": striped(np.random.permutation(U)[:S]),
        "c0": striped(near[:W]),
        "c1": striped(near[W:]),
        "c2": striped(np.random.permutation(U)[:W]),
    }


def reference(x_words, x_scales, w1_words, w1_scales, grid, rob, unit, w2_words, w2_scales, offs, gh, inn, c0, c1, c2):
    xq = unpack_weight(x_words, x_scales)[:, unstriped(offs)]
    y = unpack_fp4(w1_words, w1_scales).T @ xq
    insd = f64(grid)[:, unstriped(inn)]
    robin = 0.8 * np.tanh(y) + f64(rob) * (insd - f64(grid)[:, unstriped(gh)])
    gnew = f64(grid).copy()
    gnew[:, unstriped(gh)] = robin
    g_c1 = gnew[:, unstriped(c1)]
    g_c2 = gnew[:, unstriped(c2)]
    g_c0 = gnew[:, unstriped(c0)]
    lap = g_c1 + g_c2 - (1.6 * g_c0)
    nl = lap * np.abs(g_c0)
    hid = f64(unit) * nl
    return unpack_fp4(w2_words, w2_scales).T @ mxq(hid, 0, "e4m3")

@@ -1,0 +1,226 @@
+from contextlib import ExitStack
+
+import concourse.mybir as mybir
+
+K, T, S, N, H, U, W = 512, 1024, 512, 128, 512, 1024, 512
+FLOPS = 2 * K * H * S + 2 * H * N * W
+
+F32 = mybir.dt.float32
+BF16 = mybir.dt.bfloat16
+I32 = mybir.dt.int32
+U32 = mybir.dt.uint32
+U16 = mybir.dt.uint16
+U8 = mybir.dt.uint8
+FP8X4 = mybir.dt.float8_e4m3fn_x4
+FP4X4 = mybir.dt.float4_e2m1fn_x4
+ALU = mybir.AluOpType
+ACT = mybir.ActivationFunctionType
+
+P = 128
+PACK = 4
+HALF = 256
+
+
+def tile_picked_yhalos_abs_p_kernel(
+    tc, x_words, x_scales, w1_words, w1_scales, grid, rob, unit, w2_words, w2_scales, offs, gh, inn, c0, c1, c2, out
+):
+    nc = tc.nc
+    with ExitStack() as ctx:
+        keep = ctx.enter_context(tc.tile_pool(name="keep", bufs=1))
+        psum = ctx.enter_context(tc.psum_pool(name="psum", bufs=1))
+
+        def load_list(name, src):
+            t = keep.tile([P, S // 16], U16, name=name)
+            nc.sync.dma_start(t[:], src)
+            return t
+
+        def load_scales(tile, src):
+            for q in range(4):
+                nc.sync.dma_start(tile[32 * q : 32 * q + 4, :].bitcast(I32), src[0, 4 * q : 4 * q + 4, :].bitcast(I32))
+
+        xw = keep.tile([P, T], I32, name="xw")
+        xs = keep.tile([P, T], U8, name="xs")
+        w1w_raw = keep.tile([P, 2 * H], U8, name="w1w_raw")
+        w1s_raw = keep.tile([P, H], U8, name="w1s_raw")
+        w2w = keep.tile([P, 2 * N], U8, name="w2w", align_bytes=64)
+        w2s = keep.tile([P, N], U8, name="w2s", align_bytes=64)
+        nc.vector.memset(xs[:].bitcast(I32), 0)
+        nc.gpsimd.memset(w1s_raw[:].bitcast(I32), 0)
+        nc.gpsimd.memset(w2s[:].bitcast(I32), 0)
+
+        grid_rows = grid.rearrange("(p t) c -> t p c", t=PACK)
+        g = [keep.tile([P, U], F32, name=f"g{t}") for t in range(PACK)]
+        rob_sb = keep.tile([P, PACK], F32, name="rob_sb")
+        unit_sb = keep.tile([P, PACK], F32, name="unit_sb")
+
+        ones = keep.tile([P, S], F32, name="ones")
+        nc.vector.memset(ones[:], 1.0)
+
+        offs_sb = load_list("offs_sb", offs)
+        nc.sync.dma_start(xw[:], x_words[0].rearrange("p c r -> p (c r)").bitcast(I32))
+        load_scales(xs, x_scales)
+        inn_sb = load_list("inn_sb", inn)
+        nc.sync.dma_start(g[0][:], grid_rows[0])
+        nc.sync.dma_start(g[1][:], grid_rows[1])
+        load_scales(w1s_raw, w1_scales)
+        nc.sync.dma_start(w1w_raw[:].bitcast(I32), w1_words[0].bitcast(I32))
+        nc.sync.dma_start(g[2][:], grid_rows[2])
+        gh_sb = load_list("gh_sb", gh)
+        nc.sync.dma_start(g[3][:], grid_rows[3])
+        nc.sync.dma_start(rob_sb[:], rob.rearrange("(p t) o -> p (t o)", t=PACK))
+        c0_sb = load_list("c0_sb", c0)
+        c1_sb = load_list("c1_sb", c1)
+        c2_sb = load_list("c2_sb", c2)
+        nc.sync.dma_start(unit_sb[:], unit.rearrange("(p t) o -> p (t o)", t=PACK))
+        nc.sync.dma_start(w2w[:].bitcast(I32), w2_words[0].bitcast(I32))
+        load_scales(w2s, w2_scales)
+
+        bound = keep.tile([P, S], F32, name="bound")
+        nc.scalar.activation(bound[:], ones[:], ACT.Copy, scale=0.8)
+
+        xq = keep.tile([P, S], U32, name="xq", align_bytes=64)
+        xqs = keep.tile([P, S], U8, name="xqs", align_bytes=64)
+        nc.vector.tensor_copy(xq[:], xw[:].bitcast(U32).indirect(offs_sb[:]))
+        nc.vector.tensor_copy(xqs[:], xs[:].indirect(offs_sb[:]))
+
+        w1w = keep.tile([P, PACK, 2 * P], U8, name="w1w", align_bytes=64)
+        w1s = keep.tile([P, PACK, P], U8, name="w1s", align_bytes=64)
+        nc.vector.tensor_copy(
+            w1s[:].rearrange("p t (c i) -> p c t i", i=16),
+            w1s_raw[:].rearrange("p (c i t) -> p c t i", i=16, t=PACK),
+        )
+        nc.vector.tensor_copy(
+            w1w[:].rearrange("p t (c i b) -> p c t i b", i=8, b=2),
+            w1w_raw[:].rearrange("p (c i t b) -> p c t i b", i=8, t=PACK, b=2),
+        )
+        nrob = keep.tile([P, PACK], F32, name="nrob")
+        nc.vector.tensor_scalar(nrob[:], rob_sb[:], -1.25, None, ALU.mult)
+
+        a = [keep.tile([P, S], F32, name=f"a{t}") for t in range(PACK)]
+        d = [keep.tile([P, S], F32, name=f"d{t}") for t in range(PACK)]
+        e_tiles = [keep.tile([P, S], F32, name=f"e{t}") for t in range(3)]
+        e = [e_tiles[0], e_tiles[1], e_tiles[0], e_tiles[2]]
+        y = [psum.tile([P, S], F32, name=f"y{t}") for t in range(PACK)]
+
+        def inner(t):
+            nc.scalar.activation(a[t][:], g[t][:].indirect(inn_sb[:]), ACT.Copy)
+
+        def diff(t):
+            nc.vector.tensor_tensor(d[t][:], g[t][:].indirect(gh_sb[:]), a[t][:], ALU.subtract)
+
+        def bounded(t):
+            nc.tensor.matmul_mx(
+                out=y[t][:], lhsT=w1w[:, t, :].bitcast(FP4X4), lhsT_scale=w1s[:, t, :],
+                rhs=xq[:].bitcast(FP8X4), rhs_scale=xqs[:], start=True, stop=True,
+            )
+            nc.scalar.activation(a[t][:], y[t][:], ACT.Tanh)
+
+        def robin(t):
+            nc.vector.scalar_tensor_tensor(e[t][:], d[t][:], nrob[:, t : t + 1], a[t][:], ALU.mult, ALU.add)
+
+        def scatter_scalar(t, halves):
+            for h in halves:
+                nc.scalar.activation(
+                    g[t][:].indirect(gh_sb[:, 16 * h : 16 * (h + 1)]), e[t][:, HALF * h : HALF * (h + 1)], ACT.Copy, scale=0.8
+                )
+
+        def scatter_vector(t, lo, hi):
+            nc.vector.tensor_tensor(g[t][:].indirect(gh_sb[:, lo // 16 : hi // 16]), e[t][:, lo:hi], bound[:, lo:hi], ALU.mult)
+
+        m = [keep.tile([P, W], F32, name=f"m{t}") for t in range(PACK)]
+        mag = [keep.tile([P, W], F32, name=f"mag{t}") for t in range(PACK)]
+        s1 = [keep.tile([P, W], F32, name=f"s1{t}") for t in range(PACK)]
+        lap = [keep.tile([P, W], F32, name=f"lap{t}") for t in range(PACK)]
+        hid = keep.tile([P, 2, PACK, HALF], BF16, name="hid")
+
+        def centre(t, lo, hi):
+            nc.scalar.activation(m[t][:, lo:hi], g[t][:].indirect(c0_sb[:, lo // 16 : hi // 16]), ACT.Copy, scale=-1.6)
+
+        def magnitude(t, lo, hi):
+            nc.scalar.activation(mag[t][:, lo:hi], m[t][:, lo:hi], ACT.Abs, scale=0.625)
+
+        def first(t, lo, hi):
+            nc.vector.tensor_tensor(s1[t][:, lo:hi], g[t][:].indirect(c1_sb[:, lo // 16 : hi // 16]), m[t][:, lo:hi], ALU.add)
+
+        def second(t, lo, hi):
+            nc.vector.tensor_tensor(lap[t][:, lo:hi], g[t][:].indirect(c2_sb[:, lo // 16 : hi // 16]), s1[t][:, lo:hi], ALU.add)
+
+        def hidden(t, lo, hi):
+            nc.vector.scalar_tensor_tensor(
+                hid[:, lo // HALF : hi // HALF, t, :],
+                lap[t][:, lo:hi].rearrange("p (h w) -> p h w", w=HALF),
+                unit_sb[:, t : t + 1],
+                mag[t][:, lo:hi].rearrange("p (h w) -> p h w", w=HALF),
+                ALU.mult,
+                ALU.mult,
+            )
+
+        woven = [keep.tile([P, HALF, PACK], BF16, name=f"woven{h}", align_bytes=64) for h in range(2)]
+
+        def weave(copy, h):
+            copy(woven[h][:].rearrange("p (c i) t -> p c t i", i=4), hid[:, h].rearrange("p t (c i) -> p c t i", i=4))
+
+        def finish(h):
+            cols = slice(HALF * h, HALF * (h + 1))
+            hq = keep.tile([P, HALF], U32, name=f"hq{h}", align_bytes=64)
+            hqs = keep.tile([P, HALF], U8, name=f"hqs{h}", align_bytes=64)
+            nc.vector.quantize_mx(out=hq[:].bitcast(FP8X4), scales=hqs[:], in_=woven[h][:].rearrange("p w t -> p (w t)"))
+            acc = psum.tile([P, HALF], F32, name=f"acc{h}")
+            nc.tensor.matmul_mx(
+                out=acc[:], lhsT=w2w[:].bitcast(FP4X4), lhsT_scale=w2s[:],
+                rhs=hq[:].bitcast(FP8X4), rhs_scale=hqs[:], start=True, stop=True,
+            )
+            res = keep.tile([P, HALF], F32, name=f"res{h}")
+            nc.scalar.copy(res[:], acc[:])
+            nc.sync.dma_start(out[:, cols], res[:])
+
+        inner(0)
+        inner(1)
+        inner(2)
+        inner(3)
+        diff(0)
+        diff(1)
+        diff(2)
+        bounded(0)
+        bounded(1)
+        bounded(2)
+        robin(0)
+        diff(3)
+        bounded(3)
+        robin(1)
+        scatter_scalar(0, (0, 1))
+        scatter_vector(1, 0, W)
+        centre(0, 0, W)
+        centre(1, 0, W)
+        robin(2)
+        robin(3)
+        scatter_vector(3, 0, HALF)
+        first(0, 0, W)
+        second(0, 0, W)
+        scatter_scalar(2, (0, 1))
+        magnitude(0, 0, W)
+        first(1, 0, W)
+        second(1, 0, W)
+        hidden(0, 0, W)
+        centre(2, 0, W)
+        magnitude(1, 0, W)
+        scatter_scalar(3, (1,))
+        first(2, 0, W)
+        second(2, 0, W)
+        hidden(1, 0, W)
+        centre(3, 0, HALF)
+        magnitude(2, 0, W)
+        centre(3, HALF, W)
+        hidden(2, 0, W)
+        magnitude(3, 0, HALF)
+        magnitude(3, HALF, W)
+        first(3, 0, HALF)
+        second(3, 0, HALF)
+        hidden(3, 0, HALF)
+        weave(nc.scalar.copy, 0)
+        first(3, HALF, W)
+        second(3, HALF, W)
+        hidden(3, HALF, W)
+        finish(0)
+        weave(nc.vector.tensor_copy, 1)
+        finish(1)

@@ -18,7 +18,7 @@ ACT = mybir.ActivationFunctionType
 
 P = 128
 PACK = 4
-HALF = 256
+Q = 128
 
 
 def tile_picked_yhalos_abs_p_kernel(
@@ -66,9 +66,9 @@ def tile_picked_yhalos_abs_p_kernel(
         nc.sync.dma_start(w1w_raw[:].bitcast(I32), w1_words[0].bitcast(I32))
         nc.sync.dma_start(g[2][:], grid_rows[2])
         gh_sb = load_list("gh_sb", gh)
-        nc.sync.dma_start(g[3][:], grid_rows[3])
         nc.sync.dma_start(rob_sb[:], rob.rearrange("(p t) o -> p (t o)", t=PACK))
         c0_sb = load_list("c0_sb", c0)
+        nc.sync.dma_start(g[3][:], grid_rows[3])
         c1_sb = load_list("c1_sb", c1)
         c2_sb = load_list("c2_sb", c2)
         nc.sync.dma_start(unit_sb[:], unit.rearrange("(p t) o -> p (t o)", t=PACK))
@@ -97,9 +97,10 @@ def tile_picked_yhalos_abs_p_kernel(
         nc.vector.tensor_scalar(nrob[:], rob_sb[:], -1.25, None, ALU.mult)
 
         a = [keep.tile([P, S], F32, name=f"a{t}") for t in range(PACK)]
-        d = [keep.tile([P, S], F32, name=f"d{t}") for t in range(PACK)]
-        e_tiles = [keep.tile([P, S], F32, name=f"e{t}") for t in range(3)]
-        e = [e_tiles[0], e_tiles[1], e_tiles[0], e_tiles[2]]
+        d_tiles = [keep.tile([P, S], F32, name=f"d{t}") for t in range(2)]
+        d = d_tiles + d_tiles
+        e = [keep.tile([P, S], F32, name=f"e{t}") for t in range(PACK)]
+        th = [keep.tile([P, S], F32, name=f"th{t}") for t in range(PACK)]
         y = [psum.tile([P, S], F32, name=f"y{t}") for t in range(PACK)]
 
         def inner(t):
@@ -113,16 +114,13 @@ def tile_picked_yhalos_abs_p_kernel(
                 out=y[t][:], lhsT=w1w[:, t, :].bitcast(FP4X4), lhsT_scale=w1s[:, t, :],
                 rhs=xq[:].bitcast(FP8X4), rhs_scale=xqs[:], start=True, stop=True,
             )
-            nc.scalar.activation(a[t][:], y[t][:], ACT.Tanh)
+            nc.scalar.activation(th[t][:], y[t][:], ACT.Tanh)
 
         def robin(t):
-            nc.vector.scalar_tensor_tensor(e[t][:], d[t][:], nrob[:, t : t + 1], a[t][:], ALU.mult, ALU.add)
+            nc.vector.scalar_tensor_tensor(e[t][:], d[t][:], nrob[:, t : t + 1], th[t][:], ALU.mult, ALU.add)
 
-        def scatter_scalar(t, halves):
-            for h in halves:
-                nc.scalar.activation(
-                    g[t][:].indirect(gh_sb[:, 16 * h : 16 * (h + 1)]), e[t][:, HALF * h : HALF * (h + 1)], ACT.Copy, scale=0.8
-                )
+        def scatter_scalar(t, lo, hi):
+            nc.scalar.activation(g[t][:].indirect(gh_sb[:, lo // 16 : hi // 16]), e[t][:, lo:hi], ACT.Copy, scale=0.8)
 
         def scatter_vector(t, lo, hi):
             nc.vector.tensor_tensor(g[t][:].indirect(gh_sb[:, lo // 16 : hi // 16]), e[t][:, lo:hi], bound[:, lo:hi], ALU.mult)
@@ -131,7 +129,8 @@ def tile_picked_yhalos_abs_p_kernel(
         mag = [keep.tile([P, W], F32, name=f"mag{t}") for t in range(PACK)]
         s1 = [keep.tile([P, W], F32, name=f"s1{t}") for t in range(PACK)]
         lap = [keep.tile([P, W], F32, name=f"lap{t}") for t in range(PACK)]
-        hid = keep.tile([P, 2, PACK, HALF], BF16, name="hid")
+        hid = keep.tile([P, W // Q, PACK, Q], BF16, name="hid")
+        east = keep.tile([P, W], F32, name="east")
 
         def centre(t, lo, hi):
             nc.scalar.activation(m[t][:, lo:hi], g[t][:].indirect(c0_sb[:, lo // 16 : hi // 16]), ACT.Copy, scale=-1.6)
@@ -145,82 +144,101 @@ def tile_picked_yhalos_abs_p_kernel(
         def second(t, lo, hi):
             nc.vector.tensor_tensor(lap[t][:, lo:hi], g[t][:].indirect(c2_sb[:, lo // 16 : hi // 16]), s1[t][:, lo:hi], ALU.add)
 
+        def first_alone(t, lo, hi):
+            nc.scalar.activation(east[:, lo:hi], g[t][:].indirect(c1_sb[:, lo // 16 : hi // 16]), ACT.Copy)
+
+        def second_alone(t, lo, hi):
+            nc.vector.tensor_tensor(s1[t][:, lo:hi], g[t][:].indirect(c2_sb[:, lo // 16 : hi // 16]), m[t][:, lo:hi], ALU.add)
+
+        def join(t, lo, hi):
+            nc.vector.tensor_tensor(lap[t][:, lo:hi], s1[t][:, lo:hi], east[:, lo:hi], ALU.add)
+
         def hidden(t, lo, hi):
             nc.vector.scalar_tensor_tensor(
-                hid[:, lo // HALF : hi // HALF, t, :],
-                lap[t][:, lo:hi].rearrange("p (h w) -> p h w", w=HALF),
+                hid[:, lo // Q : hi // Q, t, :],
+                lap[t][:, lo:hi].rearrange("p (h w) -> p h w", w=Q),
                 unit_sb[:, t : t + 1],
-                mag[t][:, lo:hi].rearrange("p (h w) -> p h w", w=HALF),
+                mag[t][:, lo:hi].rearrange("p (h w) -> p h w", w=Q),
                 ALU.mult,
                 ALU.mult,
             )
 
-        woven = [keep.tile([P, HALF, PACK], BF16, name=f"woven{h}", align_bytes=64) for h in range(2)]
+        woven = [keep.tile([P, 2 * Q, PACK], BF16, name=f"woven{h}", align_bytes=64) for h in range(2)]
 
-        def weave(copy, h):
-            copy(woven[h][:].rearrange("p (c i) t -> p c t i", i=4), hid[:, h].rearrange("p t (c i) -> p c t i", i=4))
+        def weave(copy, lo, hi):
+            q = lo // Q
+            copy(
+                woven[q // 2][:, (q % 2) * Q : (q % 2 + 1) * Q, :].rearrange("p (c i) t -> p c t i", i=4),
+                hid[:, q].rearrange("p t (c i) -> p c t i", i=4),
+            )
 
-        def finish(h):
-            cols = slice(HALF * h, HALF * (h + 1))
-            hq = keep.tile([P, HALF], U32, name=f"hq{h}", align_bytes=64)
-            hqs = keep.tile([P, HALF], U8, name=f"hqs{h}", align_bytes=64)
-            nc.vector.quantize_mx(out=hq[:].bitcast(FP8X4), scales=hqs[:], in_=woven[h][:].rearrange("p w t -> p (w t)"))
-            acc = psum.tile([P, HALF], F32, name=f"acc{h}")
+        def finish(lo, hi):
+            n = hi - lo
+            hq = keep.tile([P, n], U32, name=f"hq{lo}", align_bytes=64)
+            hqs = keep.tile([P, n], U8, name=f"hqs{lo}", align_bytes=64)
+            nc.vector.quantize_mx(out=hq[:].bitcast(FP8X4), scales=hqs[:], in_=woven[lo // n][:].rearrange("p w t -> p (w t)"))
+            acc = psum.tile([P, n], F32, name=f"acc{lo}")
             nc.tensor.matmul_mx(
                 out=acc[:], lhsT=w2w[:].bitcast(FP4X4), lhsT_scale=w2s[:],
                 rhs=hq[:].bitcast(FP8X4), rhs_scale=hqs[:], start=True, stop=True,
             )
-            res = keep.tile([P, HALF], F32, name=f"res{h}")
+            res = keep.tile([P, n], F32, name=f"res{lo}")
             nc.scalar.copy(res[:], acc[:])
-            nc.sync.dma_start(out[:, cols], res[:])
+            nc.sync.dma_start(out[:, lo:hi], res[:])
 
         inner(0)
         inner(1)
         inner(2)
-        inner(3)
-        diff(0)
-        diff(1)
-        diff(2)
         bounded(0)
         bounded(1)
         bounded(2)
-        robin(0)
-        diff(3)
         bounded(3)
+        diff(0)
+        diff(1)
+        robin(0)
         robin(1)
-        scatter_scalar(0, (0, 1))
+        scatter_scalar(0, 0, 256)
+        scatter_scalar(0, 256, 512)
+        diff(2)
         scatter_vector(1, 0, W)
+        robin(2)
+        inner(3)
         centre(0, 0, W)
         centre(1, 0, W)
-        robin(2)
+        diff(3)
+        scatter_scalar(2, 0, 256)
+        scatter_scalar(2, 256, 512)
         robin(3)
-        scatter_vector(3, 0, HALF)
         first(0, 0, W)
-        second(0, 0, W)
-        scatter_scalar(2, (0, 1))
-        magnitude(0, 0, W)
         first(1, 0, W)
+        scatter_vector(3, 0, 128)
+        second(0, 0, W)
         second(1, 0, W)
-        hidden(0, 0, W)
         centre(2, 0, W)
+        magnitude(0, 0, W)
         magnitude(1, 0, W)
-        scatter_scalar(3, (1,))
+        scatter_scalar(3, 128, 512)
+        magnitude(2, 0, W)
         first(2, 0, W)
         second(2, 0, W)
+        hidden(0, 0, W)
         hidden(1, 0, W)
-        centre(3, 0, HALF)
-        magnitude(2, 0, W)
-        centre(3, HALF, W)
         hidden(2, 0, W)
-        magnitude(3, 0, HALF)
-        magnitude(3, HALF, W)
-        first(3, 0, HALF)
-        second(3, 0, HALF)
-        hidden(3, 0, HALF)
-        weave(nc.scalar.copy, 0)
-        first(3, HALF, W)
-        second(3, HALF, W)
-        hidden(3, HALF, W)
-        finish(0)
-        weave(nc.vector.tensor_copy, 1)
-        finish(1)
+        centre(3, 0, 256)
+        centre(3, 256, 512)
+        first_alone(3, 0, 256)
+        first_alone(3, 256, 512)
+        magnitude(3, 0, 256)
+        magnitude(3, 256, 512)
+        second_alone(3, 0, 256)
+        second_alone(3, 256, 512)
+        join(3, 0, 256)
+        join(3, 256, 512)
+        hidden(3, 0, 256)
+        hidden(3, 256, 512)
+        weave(nc.scalar.copy, 0, 128)
+        weave(nc.vector.tensor_copy, 128, 256)
+        weave(nc.scalar.copy, 256, 384)
+        weave(nc.vector.tensor_copy, 384, 512)
+        finish(0, 256)
+        finish(256, 512)

@@ -56,19 +56,19 @@ def tile_picked_yhalos_abs_p_kernel(
         ones = keep.tile([P, S], F32, name="ones")
         nc.vector.memset(ones[:], 1.0)
 
+        nc.sync.dma_start(w1w_raw[:].bitcast(I32), w1_words[0].bitcast(I32))
         offs_sb = load_list("offs_sb", offs)
         nc.sync.dma_start(xw[:], x_words[0].rearrange("p c r -> p (c r)").bitcast(I32))
         load_scales(xs, x_scales)
-        inn_sb = load_list("inn_sb", inn)
         nc.sync.dma_start(g[0][:], grid_rows[0])
+        inn_sb = load_list("inn_sb", inn)
         nc.sync.dma_start(g[1][:], grid_rows[1])
         load_scales(w1s_raw, w1_scales)
-        nc.sync.dma_start(w1w_raw[:].bitcast(I32), w1_words[0].bitcast(I32))
-        nc.sync.dma_start(g[2][:], grid_rows[2])
-        gh_sb = load_list("gh_sb", gh)
         nc.sync.dma_start(rob_sb[:], rob.rearrange("(p t) o -> p (t o)", t=PACK))
-        c0_sb = load_list("c0_sb", c0)
+        gh_sb = load_list("gh_sb", gh)
+        nc.sync.dma_start(g[2][:], grid_rows[2])
         nc.sync.dma_start(g[3][:], grid_rows[3])
+        c0_sb = load_list("c0_sb", c0)
         c1_sb = load_list("c1_sb", c1)
         c2_sb = load_list("c2_sb", c2)
         nc.sync.dma_start(unit_sb[:], unit.rearrange("(p t) o -> p (t o)", t=PACK))

from contextlib import ExitStack

import concourse.mybir as mybir

K, T, S, N, H, U, W = 512, 1024, 512, 128, 512, 1024, 512
FLOPS = 2 * K * H * S + 2 * H * N * W

F32 = mybir.dt.float32
BF16 = mybir.dt.bfloat16
I32 = mybir.dt.int32
U32 = mybir.dt.uint32
U16 = mybir.dt.uint16
U8 = mybir.dt.uint8
FP8X4 = mybir.dt.float8_e4m3fn_x4
FP4X4 = mybir.dt.float4_e2m1fn_x4
ALU = mybir.AluOpType
ACT = mybir.ActivationFunctionType

P = 128
PACK = 4
Q = 128


def tile_picked_yhalos_abs_p_kernel(
    tc, x_words, x_scales, w1_words, w1_scales, grid, rob, unit, w2_words, w2_scales, offs, gh, inn, c0, c1, c2, out
):
    nc = tc.nc
    with ExitStack() as ctx:
        keep = ctx.enter_context(tc.tile_pool(name="keep", bufs=1))
        psum = ctx.enter_context(tc.psum_pool(name="psum", bufs=1))

        def load_list(name, src):
            t = keep.tile([P, S // 16], U16, name=name)
            nc.sync.dma_start(t[:], src)
            return t

        def load_scales(tile, src):
            for q in range(4):
                nc.sync.dma_start(tile[32 * q : 32 * q + 4, :].bitcast(I32), src[0, 4 * q : 4 * q + 4, :].bitcast(I32))

        xw = keep.tile([P, T], I32, name="xw")
        xs = keep.tile([P, T], U8, name="xs")
        w1w_raw = keep.tile([P, 2 * H], U8, name="w1w_raw")
        w1s_raw = keep.tile([P, H], U8, name="w1s_raw")
        w2w = keep.tile([P, 2 * N], U8, name="w2w", align_bytes=64)
        w2s = keep.tile([P, N], U8, name="w2s", align_bytes=64)
        nc.vector.memset(xs[:].bitcast(I32), 0)
        nc.gpsimd.memset(w1s_raw[:].bitcast(I32), 0)
        nc.gpsimd.memset(w2s[:].bitcast(I32), 0)

        grid_rows = grid.rearrange("(p t) c -> t p c", t=PACK)
        g = [keep.tile([P, U], F32, name=f"g{t}") for t in range(PACK)]
        rob_sb = keep.tile([P, PACK], F32, name="rob_sb")
        unit_sb = keep.tile([P, PACK], F32, name="unit_sb")

        ones = keep.tile([P, S], F32, name="ones")
        nc.vector.memset(ones[:], 1.0)

        nc.sync.dma_start(w1w_raw[:].bitcast(I32), w1_words[0].bitcast(I32))
        offs_sb = load_list("offs_sb", offs)
        nc.sync.dma_start(xw[:], x_words[0].rearrange("p c r -> p (c r)").bitcast(I32))
        load_scales(xs, x_scales)
        nc.sync.dma_start(g[0][:], grid_rows[0])
        inn_sb = load_list("inn_sb", inn)
        nc.sync.dma_start(g[1][:], grid_rows[1])
        load_scales(w1s_raw, w1_scales)
        nc.sync.dma_start(rob_sb[:], rob.rearrange("(p t) o -> p (t o)", t=PACK))
        gh_sb = load_list("gh_sb", gh)
        nc.sync.dma_start(g[2][:], grid_rows[2])
        nc.sync.dma_start(g[3][:], grid_rows[3])
        c0_sb = load_list("c0_sb", c0)
        c1_sb = load_list("c1_sb", c1)
        c2_sb = load_list("c2_sb", c2)
        nc.sync.dma_start(unit_sb[:], unit.rearrange("(p t) o -> p (t o)", t=PACK))
        nc.sync.dma_start(w2w[:].bitcast(I32), w2_words[0].bitcast(I32))
        load_scales(w2s, w2_scales)

        bound = keep.tile([P, S], F32, name="bound")
        nc.scalar.activation(bound[:], ones[:], ACT.Copy, scale=0.8)

        xq = keep.tile([P, S], U32, name="xq", align_bytes=64)
        xqs = keep.tile([P, S], U8, name="xqs", align_bytes=64)
        nc.vector.tensor_copy(xq[:], xw[:].bitcast(U32).indirect(offs_sb[:]))
        nc.vector.tensor_copy(xqs[:], xs[:].indirect(offs_sb[:]))

        w1w = keep.tile([P, PACK, 2 * P], U8, name="w1w", align_bytes=64)
        w1s = keep.tile([P, PACK, P], U8, name="w1s", align_bytes=64)
        nc.vector.tensor_copy(
            w1s[:].rearrange("p t (c i) -> p c t i", i=16),
            w1s_raw[:].rearrange("p (c i t) -> p c t i", i=16, t=PACK),
        )
        nc.vector.tensor_copy(
            w1w[:].rearrange("p t (c i b) -> p c t i b", i=8, b=2),
            w1w_raw[:].rearrange("p (c i t b) -> p c t i b", i=8, t=PACK, b=2),
        )
        nrob = keep.tile([P, PACK], F32, name="nrob")
        nc.vector.tensor_scalar(nrob[:], rob_sb[:], -1.25, None, ALU.mult)

        a = [keep.tile([P, S], F32, name=f"a{t}") for t in range(PACK)]
        d_tiles = [keep.tile([P, S], F32, name=f"d{t}") for t in range(2)]
        d = d_tiles + d_tiles
        e = [keep.tile([P, S], F32, name=f"e{t}") for t in range(PACK)]
        th = [keep.tile([P, S], F32, name=f"th{t}") for t in range(PACK)]
        y = [psum.tile([P, S], F32, name=f"y{t}") for t in range(PACK)]

        def inner(t):
            nc.scalar.activation(a[t][:], g[t][:].indirect(inn_sb[:]), ACT.Copy)

        def diff(t):
            nc.vector.tensor_tensor(d[t][:], g[t][:].indirect(gh_sb[:]), a[t][:], ALU.subtract)

        def bounded(t):
            nc.tensor.matmul_mx(
                out=y[t][:], lhsT=w1w[:, t, :].bitcast(FP4X4), lhsT_scale=w1s[:, t, :],
                rhs=xq[:].bitcast(FP8X4), rhs_scale=xqs[:], start=True, stop=True,
            )
            nc.scalar.activation(th[t][:], y[t][:], ACT.Tanh)

        def robin(t):
            nc.vector.scalar_tensor_tensor(e[t][:], d[t][:], nrob[:, t : t + 1], th[t][:], ALU.mult, ALU.add)

        def scatter_scalar(t, lo, hi):
            nc.scalar.activation(g[t][:].indirect(gh_sb[:, lo // 16 : hi // 16]), e[t][:, lo:hi], ACT.Copy, scale=0.8)

        def scatter_vector(t, lo, hi):
            nc.vector.tensor_tensor(g[t][:].indirect(gh_sb[:, lo // 16 : hi // 16]), e[t][:, lo:hi], bound[:, lo:hi], ALU.mult)

        m = [keep.tile([P, W], F32, name=f"m{t}") for t in range(PACK)]
        mag = [keep.tile([P, W], F32, name=f"mag{t}") for t in range(PACK)]
        s1 = [keep.tile([P, W], F32, name=f"s1{t}") for t in range(PACK)]
        lap = [keep.tile([P, W], F32, name=f"lap{t}") for t in range(PACK)]
        hid = keep.tile([P, W // Q, PACK, Q], BF16, name="hid")
        east = keep.tile([P, W], F32, name="east")

        def centre(t, lo, hi):
            nc.scalar.activation(m[t][:, lo:hi], g[t][:].indirect(c0_sb[:, lo // 16 : hi // 16]), ACT.Copy, scale=-1.6)

        def magnitude(t, lo, hi):
            nc.scalar.activation(mag[t][:, lo:hi], m[t][:, lo:hi], ACT.Abs, scale=0.625)

        def first(t, lo, hi):
            nc.vector.tensor_tensor(s1[t][:, lo:hi], g[t][:].indirect(c1_sb[:, lo // 16 : hi // 16]), m[t][:, lo:hi], ALU.add)

        def second(t, lo, hi):
            nc.vector.tensor_tensor(lap[t][:, lo:hi], g[t][:].indirect(c2_sb[:, lo // 16 : hi // 16]), s1[t][:, lo:hi], ALU.add)

        def first_alone(t, lo, hi):
            nc.scalar.activation(east[:, lo:hi], g[t][:].indirect(c1_sb[:, lo // 16 : hi // 16]), ACT.Copy)

        def second_alone(t, lo, hi):
            nc.vector.tensor_tensor(s1[t][:, lo:hi], g[t][:].indirect(c2_sb[:, lo // 16 : hi // 16]), m[t][:, lo:hi], ALU.add)

        def join(t, lo, hi):
            nc.vector.tensor_tensor(lap[t][:, lo:hi], s1[t][:, lo:hi], east[:, lo:hi], ALU.add)

        def hidden(t, lo, hi):
            nc.vector.scalar_tensor_tensor(
                hid[:, lo // Q : hi // Q, t, :],
                lap[t][:, lo:hi].rearrange("p (h w) -> p h w", w=Q),
                unit_sb[:, t : t + 1],
                mag[t][:, lo:hi].rearrange("p (h w) -> p h w", w=Q),
                ALU.mult,
                ALU.mult,
            )

        woven = [keep.tile([P, 2 * Q, PACK], BF16, name=f"woven{h}", align_bytes=64) for h in range(2)]

        def weave(copy, lo, hi):
            q = lo // Q
            copy(
                woven[q // 2][:, (q % 2) * Q : (q % 2 + 1) * Q, :].rearrange("p (c i) t -> p c t i", i=4),
                hid[:, q].rearrange("p t (c i) -> p c t i", i=4),
            )

        def finish(lo, hi):
            n = hi - lo
            hq = keep.tile([P, n], U32, name=f"hq{lo}", align_bytes=64)
            hqs = keep.tile([P, n], U8, name=f"hqs{lo}", align_bytes=64)
            nc.vector.quantize_mx(out=hq[:].bitcast(FP8X4), scales=hqs[:], in_=woven[lo // n][:].rearrange("p w t -> p (w t)"))
            acc = psum.tile([P, n], F32, name=f"acc{lo}")
            nc.tensor.matmul_mx(
                out=acc[:], lhsT=w2w[:].bitcast(FP4X4), lhsT_scale=w2s[:],
                rhs=hq[:].bitcast(FP8X4), rhs_scale=hqs[:], start=True, stop=True,
            )
            res = keep.tile([P, n], F32, name=f"res{lo}")
            nc.scalar.copy(res[:], acc[:])
            nc.sync.dma_start(out[:, lo:hi], res[:])

        inner(0)
        inner(1)
        inner(2)
        bounded(0)
        bounded(1)
        bounded(2)
        bounded(3)
        diff(0)
        diff(1)
        robin(0)
        robin(1)
        scatter_scalar(0, 0, 256)
        scatter_scalar(0, 256, 512)
        diff(2)
        scatter_vector(1, 0, W)
        robin(2)
        inner(3)
        centre(0, 0, W)
        centre(1, 0, W)
        diff(3)
        scatter_scalar(2, 0, 256)
        scatter_scalar(2, 256, 512)
        robin(3)
        first(0, 0, W)
        first(1, 0, W)
        scatter_vector(3, 0, 128)
        second(0, 0, W)
        second(1, 0, W)
        centre(2, 0, W)
        magnitude(0, 0, W)
        magnitude(1, 0, W)
        scatter_scalar(3, 128, 512)
        magnitude(2, 0, W)
        first(2, 0, W)
        second(2, 0, W)
        hidden(0, 0, W)
        hidden(1, 0, W)
        hidden(2, 0, W)
        centre(3, 0, 256)
        centre(3, 256, 512)
        first_alone(3, 0, 256)
        first_alone(3, 256, 512)
        magnitude(3, 0, 256)
        magnitude(3, 256, 512)
        second_alone(3, 0, 256)
        second_alone(3, 256, 512)
        join(3, 0, 256)
        join(3, 256, 512)
        hidden(3, 0, 256)
        hidden(3, 256, 512)
        weave(nc.scalar.copy, 0, 128)
        weave(nc.vector.tensor_copy, 128, 256)
        weave(nc.scalar.copy, 256, 384)
        weave(nc.vector.tensor_copy, 384, 512)
        finish(0, 256)
        finish(256, 512)
